import numpy as np
import ml_dtypes


def mxq(x, axis, fmt="e4m3"):
    dtype, down = {"e4m3": (ml_dtypes.float8_e4m3fn, 7), "e5m2": (ml_dtypes.float8_e5m2, 14)}[fmt]
    v = np.moveaxis(np.asarray(x, np.float32).astype(ml_dtypes.bfloat16).astype(np.float64), axis, -1)
    blocks = v.reshape(v.shape[:-1] + (-1, 32))
    amax = np.abs(blocks).max(-1, keepdims=True)
    byte = np.maximum(np.where(amax > 0, np.frexp(amax)[1] - 1 + 127, 0) - down, 1)
    scale = np.exp2(byte - 127.0)
    codes = (blocks / scale).astype(np.float32).astype(dtype).astype(np.float64)
    return np.moveaxis((codes * scale).reshape(v.shape), -1, axis)


WIDE = False


def mx_kscale(k):
    if not WIDE:
        return np.ones(k)
    levels = np.array([10, -10, 5, -5, 0])
    if k % 512:
        return np.exp2(np.random.permutation(np.resize(levels, k // 32))).repeat(32)
    a = np.empty((k // 512, 16))
    for p in range(k // 512):
        a[p, :8] = np.random.permutation(np.resize(levels, 8))
        for g in range(8):
            far = levels[np.abs(levels - a[p, g]) >= 10]
            a[p, g + 8] = far[np.random.randint(len(far))]
    return np.exp2(a.ravel()).repeat(32)


def f64(x):
    return np.asarray(x).astype(np.float64)


E2M1 = np.array([0.0, 0.5, 1.0, 1.5, 2.0, 3.0, 4.0, 6.0, -0.0, -0.5, -1.0, -1.5, -2.0, -3.0, -4.0, -6.0])


def pack_weight(w, fmt):
    k, n = w.shape
    w = f64(np.asarray(w, np.float32).astype(ml_dtypes.bfloat16)).reshape(k // 32, 32, n)
    amax = np.abs(w).max(1)
    if fmt == "e4m3":
        byte = np.frexp(amax)[1] - 1 + 127 - 7
    else:
        mant, ex = np.frexp(amax / 6.0)
        byte = np.where(mant > 0.5, ex, ex - 1) + 127
    byte = np.clip(np.where(amax > 0, byte, 1), 1, 254)
    scaled = (w * np.exp2(127.0 - byte)[:, None, :]).reshape(k, n).astype(np.float32)
    by_word = np.ascontiguousarray(scaled.reshape(k // 512, 128, 4, n).transpose(0, 1, 3, 2))
    if fmt == "e4m3":
        words = by_word.astype(ml_dtypes.float8_e4m3fn).view(np.uint8)
    else:
        c = by_word.astype(ml_dtypes.float4_e2m1fn).view(np.uint8) & 0xF
        words = (c[..., 0::2] | (c[..., 1::2] << 4)).reshape(k // 512, 128, 2 * n)
    return np.ascontiguousarray(words), np.ascontiguousarray(byte.astype(np.uint8).reshape(k // 512, 16, n))


def unpack_weight(words, scales, fmt):
    g, _, n = scales.shape
    words = np.ascontiguousarray(words).reshape(g, 128, n, -1)
    if fmt == "e4m3":
        vals = words.view(ml_dtypes.float8_e4m3fn).astype(np.float64)
    else:
        nib = np.empty((g, 128, n, 4), np.uint8)
        nib[..., 0::2] = words & 0xF
        nib[..., 1::2] = words >> 4
        vals = E2M1[nib]
    vals = vals * np.repeat(np.exp2(scales.astype(np.float64) - 127.0), 8, axis=1)[..., None]
    return vals.transpose(0, 1, 3, 2).reshape(g * 512, n)


def planes(y):
    n, m = y.shape
    v = y.astype(np.float32).astype(ml_dtypes.bfloat16).astype(np.float64).reshape(n // 32, 32, m)
    top = np.abs(v).max(1)
    byte = np.clip(np.where(top > 0, np.frexp(top)[1] - 1 + 127 - 7, 1), 1, 254)
    codes = (v * np.exp2(127.0 - byte)[:, None, :]).reshape(n, m).astype(np.float32).astype(ml_dtypes.float8_e4m3fn).view(np.uint8)
    words = codes.reshape(n // 512, 128, 4, m).transpose(0, 1, 3, 2)
    return np.ascontiguousarray(words), np.ascontiguousarray(byte.astype(np.uint8).reshape(n // 512, 16, m))


O, K, M, T = 1024, 2048, 1024, 512


def setup_inputs():
    n = np.random.standard_normal
    s = mx_kscale(K)[:, None]
    x = n((K, T)); x[:O] *= 6.0
    w = n((K, M)) / np.sqrt(K) / s; w[:O] /= 2.0
    p_w8 = pack_weight(w[:O], "e4m3")
    p_w4 = pack_weight(w[O:], "e2m1")
    return {
        "x": (x * s).astype(np.float32),
        "w8_words": p_w8[0],
        "w8_scales": p_w8[1],
        "w4_words": p_w4[0],
        "w4_scales": p_w4[1],
    }


def reference(x, w8_words, w8_scales, w4_words, w4_scales):
    x_ = mxq(f64(x), 0, "e4m3")
    w8_ = unpack_weight(w8_words, w8_scales, "e4m3")
    w4_ = unpack_weight(w4_words, w4_scales, "e2m1")
    y = w8_.T @ x_[:O] + w4_.T @ x_[O:]
    out_0 = y
    return (out_0,) + planes(out_0)

@@ -1,0 +1,242 @@
+from contextlib import ExitStack
+
+import concourse.mybir as mybir
+
+K, M, T = 2048, 1024, 512
+FLOPS = 2 * K * M * T
+
+F32 = mybir.dt.float32
+BF16 = mybir.dt.bfloat16
+I32 = mybir.dt.int32
+U32 = mybir.dt.uint32
+U8 = mybir.dt.uint8
+FP8X4 = mybir.dt.float8_e4m3fn_x4
+FP4X4 = mybir.dt.float4_e2m1fn_x4
+
+P = 128
+PACK = 4
+TC = 256
+NB = 128
+
+
+def tile_mix_outl_fm_pl_none_kernel(
+    tc, x, w8_words, w8_scales, w4_words, w4_scales, out_0, out_1, out_2
+):
+    nc = tc.nc
+    x_v = x.rearrange("(g p j) t -> g p j t", p=P, j=PACK)
+    y_v = out_0.rearrange("(a p r) t -> a p r t", p=P, r=PACK)
+    w8_v = w8_words.rearrange("g p n i -> g p (n i)").bitcast(I32)
+    w4_v = w4_words.bitcast(I32)
+    s8_v = w8_scales.bitcast(I32)
+    s4_v = w4_scales.bitcast(I32).rearrange("g (q r) n -> r q g n", r=4)
+    codes_v = out_1.rearrange("a p t i -> p a (t i)").bitcast(I32)
+    scales_v = out_2.bitcast(I32).rearrange("a (q r) t -> r q a t", r=4)
+
+    with ExitStack() as ctx:
+        sb = ctx.enter_context(tc.tile_pool(name="sb", bufs=1))
+        ps = ctx.enter_context(tc.psum_pool(name="ps", bufs=1))
+
+        def sbt(shape, dtype, name):
+            return sb.tile(shape, dtype, name=name, align_bytes=64)
+
+        w4_raw = [sbt([P, 2 * M], U8, "w4_raw%d" % g) for g in range(2)]
+        w4 = [sbt([P, 2 * M], U8, "w4_%d" % g) for g in range(2)]
+        w8_raw = [sbt([P, M], U32, "w8_raw%d" % g) for g in range(2)]
+        w8 = [sbt([P, M], U32, "w8_%d" % g) for g in range(2)]
+        s4_raw = sbt([P, 2, M], U8, "s4_raw")
+        s4 = [sbt([P, M], U8, "s4_%d" % g) for g in range(2)]
+        s8_raw = sbt([P, M], U8, "s8_raw")
+        s8 = sbt([P, M], U8, "s8")
+        keys = [(g, c) for g in range(4) for c in range(2)]
+        x_raw = {k: sbt([P, PACK, TC], F32, "x_raw%d%d" % k) for k in keys}
+        x_bf = {k: sbt([P, TC, PACK], BF16, "x_bf%d%d" % k) for k in keys}
+        x_codes = {k: sbt([P, TC], U32, "x_codes%d%d" % k) for k in keys}
+        x_scales = {k: sbt([P, TC], U8, "x_scales%d%d" % k) for k in keys}
+        ca = [(c, a) for c in range(2) for a in range(2)]
+        y_f32 = {k: sbt([P, PACK, TC], F32, "y_f32%d%d" % k) for k in ca}
+        y_bf = {k: sbt([P, TC, PACK], BF16, "y_bf%d%d" % k) for k in ca}
+        y_codes = [sbt([P, 2, TC], U32, "y_codes%d" % c) for c in range(2)]
+        y_scales = sbt([P, 2, T], U8, "y_scales")
+        banks = {(c, a, h): ps.tile([P, 2, TC], F32, name="bank%d%d%d" % (c, a, h))
+                 for c in range(2) for a in range(2) for h in range(2)}
+
+        def tok(c):
+            return slice(c * TC, (c + 1) * TC)
+
+        def load_x(g, c):
+            nc.sync.dma_start(out=x_raw[(g, c)][:], in_=x_v[g][:, :, tok(c)])
+
+        def load_w4(g):
+            nc.sync.dma_start(out=w4_raw[g][:].bitcast(I32), in_=w4_v[g])
+
+        def load_w8(g):
+            nc.sync.dma_start(out=w8_raw[g][:].bitcast(I32), in_=w8_v[g])
+
+        def load_s4(eng):
+            view = s4_raw[:].bitcast(I32)
+            for r in range(4):
+                eng.dma_start(out=view[r:P:32], in_=s4_v[r])
+
+        def load_s8(eng):
+            view = s8_raw[:].bitcast(I32)
+            for q in range(4):
+                eng.dma_start(out=view[32 * q + 4 : 32 * q + 12, :], in_=s8_v[:, 4 * q : 4 * q + 4, :])
+
+        def deal(dst, src, width):
+            nc.vector.tensor_copy(
+                out=dst.rearrange("p (r m b) -> p r m b", r=PACK, b=width),
+                in_=src.rearrange("p (m r b) -> p r m b", r=PACK, b=width),
+            )
+
+        def deal1(dst, src):
+            nc.vector.tensor_copy(
+                out=dst.rearrange("p (r m) -> p r m", r=PACK),
+                in_=src.rearrange("p (m r) -> p r m", r=PACK),
+            )
+
+        def interleave(dst, src, v_cols):
+            for lo, hi, copy in ((0, v_cols, nc.vector.tensor_copy), (v_cols, TC, nc.scalar.copy)):
+                if hi > lo:
+                    copy(
+                        out=dst[:, lo:hi, :].rearrange("p (c i) j -> p c j i", i=4),
+                        in_=src[:, :, lo:hi].rearrange("p j (c i) -> p c j i", i=4),
+                    )
+
+        def il_x(g, c, v_cols):
+            interleave(x_bf[(g, c)], x_raw[(g, c)], v_cols)
+
+        def quant_x(g, c):
+            nc.vector.quantize_mx(
+                out=x_codes[(g, c)][:].bitcast(FP8X4),
+                scales=x_scales[(g, c)][:],
+                in_=x_bf[(g, c)][:].rearrange("p t j -> p (t j)"),
+            )
+
+        def il_y(c, a, v_cols):
+            interleave(y_bf[(c, a)], y_f32[(c, a)], v_cols)
+
+        def quant_y(c, a):
+            nc.vector.quantize_mx(
+                out=y_codes[c][:, a, :].bitcast(FP8X4),
+                scales=y_scales[:, a, tok(c)],
+                in_=y_bf[(c, a)][:].rearrange("p t j -> p (t j)"),
+            )
+
+        def matmuls(g, c):
+            for a in range(2):
+                for r in range(PACK):
+                    col = r * 256 + a * P
+                    out = banks[(c, a, r // 2)][:, r % 2, :]
+                    if g >= 2:
+                        for lo in range(0, TC, NB):
+                            nc.tensor.matmul_mx(
+                                out=out[:, lo : lo + NB],
+                                lhsT=w4[g - 2][:, 2 * col : 2 * (col + P)].bitcast(FP4X4),
+                                lhsT_scale=s4[g - 2][:, col : col + P],
+                                rhs=x_codes[(g, c)][:, lo : lo + NB].bitcast(FP8X4),
+                                rhs_scale=x_scales[(g, c)][:, lo : lo + NB],
+                                start=(g == 2 and r % 2 == 0 and lo == 0),
+                                stop=False,
+                            )
+                    else:
+                        nc.tensor.matmul_mx(
+                            out=out,
+                            lhsT=w8[g][:, col : col + P].bitcast(FP8X4),
+                            lhsT_scale=s8[4 + 4 * g : P, col : col + P],
+                            rhs=x_codes[(g, c)][:].bitcast(FP8X4),
+                            rhs_scale=x_scales[(g, c)][:],
+                            start=False,
+                            stop=(g == 1 and r % 2 == 1),
+                        )
+
+        def evac(c, a, h, copy):
+            copy(out=y_f32[(c, a)][:, 2 * h : 2 * h + 2, :], in_=banks[(c, a, h)][:])
+
+        def store_y(c, a, lo, hi):
+            nc.sync.dma_start(out=y_v[a][:, lo:hi, tok(c)], in_=y_f32[(c, a)][:, lo:hi, :])
+
+        def store_codes(c, lo, hi):
+            nc.sync.dma_start(out=codes_v[:, lo:hi, tok(c)], in_=y_codes[c][:, lo:hi, :].bitcast(I32))
+
+        def store_scales():
+            view = y_scales[:].bitcast(I32)
+            for r in range(4):
+                eng = nc.scalar if r % 2 == 0 else nc.sync
+                eng.dma_start(out=scales_v[r], in_=view[r:P:32])
+
+        s_copy = nc.scalar.copy
+        v_copy = nc.vector.tensor_copy
+
+        with tc.manual_schedule():
+            nc.vector.memset(s4_raw[:].bitcast(I32), 0)
+            nc.vector.memset(s8_raw[:].bitcast(I32), 0)
+            load_w4(0)
+            load_x(2, 0)
+            load_s4(nc.sync)
+            load_x(2, 1)
+            load_w4(1)
+            load_x(3, 0)
+            load_w8(0)
+            load_s8(nc.sync)
+            load_x(0, 0)
+            load_w8(1)
+            load_x(1, 0)
+            load_x(3, 1)
+            load_x(0, 1)
+            load_x(1, 1)
+
+            deal(w4[0][:], w4_raw[0][:], 2)
+            deal1(s4[0][:], s4_raw[:, 0, :])
+            il_x(2, 0, 96)
+            quant_x(2, 0)
+            matmuls(2, 0)
+            il_x(2, 1, 0)
+            deal1(s4[1][:], s4_raw[:, 1, :])
+            deal(w4[1][:], w4_raw[1][:], 2)
+            quant_x(2, 1)
+            matmuls(2, 1)
+            il_x(3, 0, 0)
+            deal1(s8[:], s8_raw[:])
+            quant_x(3, 0)
+            matmuls(3, 0)
+            deal1(w8[0][:].bitcast(I32), w8_raw[0][:].bitcast(I32))
+            il_x(0, 0, 128)
+            quant_x(0, 0)
+            matmuls(0, 0)
+            deal1(w8[1][:].bitcast(I32), w8_raw[1][:].bitcast(I32))
+            il_x(1, 0, 160)
+            quant_x(1, 0)
+            matmuls(1, 0)
+            il_x(3, 1, TC)
+            quant_x(3, 1)
+            matmuls(3, 1)
+            for a in range(2):
+                evac(0, a, 0, s_copy)
+                evac(0, a, 1, s_copy)
+                store_y(0, a, 0, 4)
+            il_x(0, 1, TC)
+            quant_x(0, 1)
+            matmuls(0, 1)
+            il_x(1, 1, 160)
+            quant_x(1, 1)
+            matmuls(1, 1)
+            il_y(0, 1, TC)
+            il_y(0, 0, 0)
+            quant_y(0, 1)
+            quant_y(0, 0)
+            evac(1, 0, 0, s_copy)
+            store_y(1, 0, 0, 2)
+            store_codes(0, 0, 2)
+            evac(1, 0, 1, v_copy)
+            evac(1, 1, 0, s_copy)
+            store_y(1, 1, 0, 2)
+            store_y(1, 0, 2, 4)
+            evac(1, 1, 1, s_copy)
+            store_y(1, 1, 2, 4)
+            il_y(1, 0, TC)
+            il_y(1, 1, 160)
+            quant_y(1, 0)
+            store_codes(1, 0, 1)
+            quant_y(1, 1)
+            store_codes(1, 1, 2)
+            store_scales()

@@ -94,16 +94,21 @@ def tile_mix_outl_fm_pl_none_kernel(
                 in_=src.rearrange("p (m r) -> p r m", r=PACK),
             )
 
-        def interleave(dst, src, v_cols):
-            for lo, hi, copy in ((0, v_cols, nc.vector.tensor_copy), (v_cols, TC, nc.scalar.copy)):
-                if hi > lo:
-                    copy(
-                        out=dst[:, lo:hi, :].rearrange("p (c i) j -> p c j i", i=4),
-                        in_=src[:, :, lo:hi].rearrange("p j (c i) -> p c j i", i=4),
-                    )
+        def interleave(dst, src, lo, hi, copy):
+            copy(
+                out=dst[:, lo:hi, :].rearrange("p (c i) j -> p c j i", i=2),
+                in_=src[:, :, lo:hi].rearrange("p j (c i) -> p c j i", i=2),
+            )
 
-        def il_x(g, c, v_cols):
-            interleave(x_bf[(g, c)], x_raw[(g, c)], v_cols)
+        def il_x(g, c, lo, hi, copy):
+            interleave(x_bf[(g, c)], x_raw[(g, c)], lo, hi, copy)
+
+        def deal_w8(g, a):
+            cols = slice(a * 512, (a + 1) * 512)
+            nc.vector.tensor_copy(
+                out=w8[g][:, cols].bitcast(I32).rearrange("p (r m) -> p m r", r=PACK),
+                in_=w8_raw[g][:, cols].bitcast(I32).rearrange("p (m r) -> p m r", r=PACK),
+            )
 
         def quant_x(g, c):
             nc.vector.quantize_mx(
@@ -112,8 +117,8 @@ def tile_mix_outl_fm_pl_none_kernel(
                 in_=x_bf[(g, c)][:].rearrange("p t j -> p (t j)"),
             )
 
-        def il_y(c, a, v_cols):
-            interleave(y_bf[(c, a)], y_f32[(c, a)], v_cols)
+        def il_y(c, a, lo, hi, copy):
+            interleave(y_bf[(c, a)], y_f32[(c, a)], lo, hi, copy)
 
         def quant_y(c, a):
             nc.vector.quantize_mx(
@@ -141,7 +146,7 @@ def tile_mix_outl_fm_pl_none_kernel(
                     else:
                         nc.tensor.matmul_mx(
                             out=out,
-                            lhsT=w8[g][:, col : col + P].bitcast(FP8X4),
+                            lhsT=w8[g][:, a * 512 + r * P : a * 512 + (r + 1) * P].bitcast(FP8X4),
                             lhsT_scale=s8[4 + 4 * g : P, col : col + P],
                             rhs=x_codes[(g, c)][:].bitcast(FP8X4),
                             rhs_scale=x_scales[(g, c)][:],
@@ -168,75 +173,83 @@ def tile_mix_outl_fm_pl_none_kernel(
         v_copy = nc.vector.tensor_copy
 
         with tc.manual_schedule():
-            nc.vector.memset(s4_raw[:].bitcast(I32), 0)
-            nc.vector.memset(s8_raw[:].bitcast(I32), 0)
             load_w4(0)
             load_x(2, 0)
+            il_x(2, 0, 96, 256, s_copy)
+            nc.vector.memset(s4_raw[:].bitcast(I32), 0)
+            nc.vector.memset(s8_raw[:].bitcast(I32), 0)
+            deal(w4[0][:], w4_raw[0][:], 2)
+            il_x(2, 0, 0, 96, v_copy)
             load_s4(nc.sync)
             load_x(2, 1)
-            load_w4(1)
             load_x(3, 0)
-            load_w8(0)
+            load_w4(1)
             load_s8(nc.sync)
             load_x(0, 0)
-            load_w8(1)
             load_x(1, 0)
+            load_w8(0)
+            load_w8(1)
             load_x(3, 1)
             load_x(0, 1)
             load_x(1, 1)
-
-            deal(w4[0][:], w4_raw[0][:], 2)
+            il_x(2, 1, 0, 256, s_copy)
+            il_x(3, 0, 0, 256, s_copy)
+            il_x(0, 0, 0, 256, s_copy)
+            il_x(1, 0, 0, 256, s_copy)
+            il_x(3, 1, 128, 256, s_copy)
             deal1(s4[0][:], s4_raw[:, 0, :])
-            il_x(2, 0, 96)
             quant_x(2, 0)
-            matmuls(2, 0)
-            il_x(2, 1, 0)
             deal1(s4[1][:], s4_raw[:, 1, :])
-            deal(w4[1][:], w4_raw[1][:], 2)
             quant_x(2, 1)
-            matmuls(2, 1)
-            il_x(3, 0, 0)
-            deal1(s8[:], s8_raw[:])
+            deal(w4[1][:], w4_raw[1][:], 2)
             quant_x(3, 0)
-            matmuls(3, 0)
-            deal1(w8[0][:].bitcast(I32), w8_raw[0][:].bitcast(I32))
-            il_x(0, 0, 128)
+            deal1(s8[:], s8_raw[:])
             quant_x(0, 0)
-            matmuls(0, 0)
-            deal1(w8[1][:].bitcast(I32), w8_raw[1][:].bitcast(I32))
-            il_x(1, 0, 160)
+            deal_w8(0, 0)
+            deal_w8(0, 1)
             quant_x(1, 0)
+            deal_w8(1, 0)
+            deal_w8(1, 1)
+            il_x(3, 1, 0, 128, v_copy)
+            matmuls(2, 0)
+            matmuls(2, 1)
+            matmuls(3, 0)
+            matmuls(0, 0)
             matmuls(1, 0)
-            il_x(3, 1, TC)
+            evac(0, 0, 0, s_copy)
+            evac(0, 1, 1, s_copy)
+            evac(0, 1, 0, s_copy)
+            evac(0, 0, 1, v_copy)
             quant_x(3, 1)
-            matmuls(3, 1)
-            for a in range(2):
-                evac(0, a, 0, s_copy)
-                evac(0, a, 1, s_copy)
-                store_y(0, a, 0, 4)
-            il_x(0, 1, TC)
+            il_x(0, 1, 0, 256, v_copy)
+            il_y(0, 0, 0, 160, v_copy)
             quant_x(0, 1)
-            matmuls(0, 1)
-            il_x(1, 1, 160)
+            il_x(1, 1, 0, 256, v_copy)
             quant_x(1, 1)
+            store_y(0, 0, 0, 4)
+            store_y(0, 1, 0, 4)
+            matmuls(3, 1)
+            matmuls(0, 1)
             matmuls(1, 1)
-            il_y(0, 1, TC)
-            il_y(0, 0, 0)
-            quant_y(0, 1)
-            quant_y(0, 0)
+            il_y(0, 0, 160, 256, s_copy)
+            il_y(0, 1, 0, 256, s_copy)
             evac(1, 0, 0, s_copy)
-            store_y(1, 0, 0, 2)
-            store_codes(0, 0, 2)
-            evac(1, 0, 1, v_copy)
             evac(1, 1, 0, s_copy)
-            store_y(1, 1, 0, 2)
+            quant_y(0, 0)
+            quant_y(0, 1)
+            evac(1, 0, 1, v_copy)
+            evac(1, 1, 1, v_copy)
+            il_y(1, 0, 0, 160, v_copy)
+            il_y(1, 1, 0, 128, v_copy)
+            store_codes(0, 0, 2)
+            store_y(1, 0, 0, 2)
             store_y(1, 0, 2, 4)
-            evac(1, 1, 1, s_copy)
             store_y(1, 1, 2, 4)
-            il_y(1, 0, TC)
-            il_y(1, 1, 160)
+            store_y(1, 1, 0, 2)
+            il_y(1, 0, 160, 256, s_copy)
+            il_y(1, 1, 128, 256, s_copy)
             quant_y(1, 0)
-            store_codes(1, 0, 1)
             quant_y(1, 1)
+            store_codes(1, 0, 1)
             store_codes(1, 1, 2)
             store_scales()

@@ -17,6 +17,7 @@ P = 128
 PACK = 4
 TC = 256
 NB = 128
+NA = 512
 
 
 def tile_mix_outl_fm_pl_none_kernel(
@@ -25,11 +26,11 @@ def tile_mix_outl_fm_pl_none_kernel(
     nc = tc.nc
     x_v = x.rearrange("(g p j) t -> g p j t", p=P, j=PACK)
     y_v = out_0.rearrange("(a p r) t -> a p r t", p=P, r=PACK)
-    w8_v = w8_words.rearrange("g p n i -> g p (n i)").bitcast(I32)
+    w8_v = w8_words.rearrange("g p n i -> p g (n i)").bitcast(I32)
     w4_v = w4_words.bitcast(I32)
     s8_v = w8_scales.bitcast(I32)
     s4_v = w4_scales.bitcast(I32).rearrange("g (q r) n -> r q g n", r=4)
-    codes_v = out_1.rearrange("a p t i -> p a (t i)").bitcast(I32)
+    codes_v = out_1.rearrange("a p t i -> a p (t i)").bitcast(I32)
     scales_v = out_2.bitcast(I32).rearrange("a (q r) t -> r q a t", r=4)
 
     with ExitStack() as ctx:
@@ -39,38 +40,44 @@ def tile_mix_outl_fm_pl_none_kernel(
         def sbt(shape, dtype, name):
             return sb.tile(shape, dtype, name=name, align_bytes=64)
 
+        def tok(c):
+            return slice(c * TC, (c + 1) * TC)
+
+        pairs = [(i, j) for i in range(2) for j in range(2)]
         w4_raw = [sbt([P, 2 * M], U8, "w4_raw%d" % g) for g in range(2)]
         w4 = [sbt([P, 2 * M], U8, "w4_%d" % g) for g in range(2)]
-        w8_raw = [sbt([P, M], U32, "w8_raw%d" % g) for g in range(2)]
-        w8 = [sbt([P, M], U32, "w8_%d" % g) for g in range(2)]
+        w8_raw = [sbt([P, 2, NA], U32, "w8_raw%d" % a) for a in range(2)]
+        w8 = {k: sbt([P, NA], U32, "w8_%d%d" % k) for k in pairs}
         s4_raw = sbt([P, 2, M], U8, "s4_raw")
         s4 = [sbt([P, M], U8, "s4_%d" % g) for g in range(2)]
         s8_raw = sbt([P, M], U8, "s8_raw")
         s8 = sbt([P, M], U8, "s8")
-        keys = [(g, c) for g in range(4) for c in range(2)]
-        x_raw = {k: sbt([P, PACK, TC], F32, "x_raw%d%d" % k) for k in keys}
-        x_bf = {k: sbt([P, TC, PACK], BF16, "x_bf%d%d" % k) for k in keys}
-        x_codes = {k: sbt([P, TC], U32, "x_codes%d%d" % k) for k in keys}
-        x_scales = {k: sbt([P, TC], U8, "x_scales%d%d" % k) for k in keys}
-        ca = [(c, a) for c in range(2) for a in range(2)]
-        y_f32 = {k: sbt([P, PACK, TC], F32, "y_f32%d%d" % k) for k in ca}
-        y_bf = {k: sbt([P, TC, PACK], BF16, "y_bf%d%d" % k) for k in ca}
-        y_codes = [sbt([P, 2, TC], U32, "y_codes%d" % c) for c in range(2)]
+        x_full = {g: sbt([P, PACK, T], F32, "x_full%d" % g) for g in (0, 2, 3)}
+        x_half = [sbt([P, PACK, TC], F32, "x_half%d" % c) for c in range(2)]
+        x_raw = {(g, c): x_full[g][:, :, tok(c)] for g in x_full for c in range(2)}
+        x_raw = dict(list(x_raw.items()) + [((1, c), x_half[c][:]) for c in range(2)])
+        x_bf = [sbt([P, T, PACK], BF16, "x_bf%d" % g) for g in range(4)]
+        x_codes = [sbt([P, T], U32, "x_codes%d" % g) for g in range(4)]
+        x_scales = [sbt([P, T], U8, "x_scales%d" % g) for g in range(4)]
+        y0_f32 = [sbt([P, PACK, TC], F32, "y0_f32%d" % c) for c in range(2)]
+        y1_f32 = sbt([P, PACK, T], F32, "y1_f32")
+        y_bf = [sbt([P, T, PACK], BF16, "y_bf%d" % a) for a in range(2)]
+        y_codes = [sbt([P, T], U32, "y_codes%d" % a) for a in range(2)]
         y_scales = sbt([P, 2, T], U8, "y_scales")
-        banks = {(c, a, h): ps.tile([P, 2, TC], F32, name="bank%d%d%d" % (c, a, h))
-                 for c in range(2) for a in range(2) for h in range(2)}
+        banks0 = {k: ps.tile([P, 2, TC], F32, name="bank0_%d%d" % k) for k in pairs}
+        banks1 = [ps.tile([P, T], F32, name="bank1_%d" % r) for r in range(PACK)]
 
-        def tok(c):
-            return slice(c * TC, (c + 1) * TC)
+        def load_x_full(g):
+            nc.sync.dma_start(out=x_full[g][:], in_=x_v[g])
 
-        def load_x(g, c):
-            nc.sync.dma_start(out=x_raw[(g, c)][:], in_=x_v[g][:, :, tok(c)])
+        def load_x_half(c):
+            nc.sync.dma_start(out=x_half[c][:], in_=x_v[1][:, :, tok(c)])
 
         def load_w4(g):
             nc.sync.dma_start(out=w4_raw[g][:].bitcast(I32), in_=w4_v[g])
 
-        def load_w8(g):
-            nc.sync.dma_start(out=w8_raw[g][:].bitcast(I32), in_=w8_v[g])
+        def load_w8(a):
+            nc.sync.dma_start(out=w8_raw[a][:].bitcast(I32), in_=w8_v[:, :, a * NA : (a + 1) * NA])
 
         def load_s4(eng):
             view = s4_raw[:].bitcast(I32)
@@ -82,16 +89,22 @@ def tile_mix_outl_fm_pl_none_kernel(
             for q in range(4):
                 eng.dma_start(out=view[32 * q + 4 : 32 * q + 12, :], in_=s8_v[:, 4 * q : 4 * q + 4, :])
 
-        def deal(dst, src, width):
+        def deal_w4(g):
             nc.vector.tensor_copy(
-                out=dst.rearrange("p (r m b) -> p r m b", r=PACK, b=width),
-                in_=src.rearrange("p (m r b) -> p r m b", r=PACK, b=width),
+                out=w4[g][:].rearrange("p (r m b) -> p r m b", r=PACK, b=2),
+                in_=w4_raw[g][:].rearrange("p (m r b) -> p r m b", r=PACK, b=2),
             )
 
-        def deal1(dst, src):
+        def deal_scales(dst, src):
             nc.vector.tensor_copy(
                 out=dst.rearrange("p (r m) -> p r m", r=PACK),
                 in_=src.rearrange("p (m r) -> p r m", r=PACK),
+            )
+
+        def deal_w8(g, a):
+            nc.vector.tensor_copy(
+                out=w8[(g, a)][:].bitcast(I32).rearrange("p (r m) -> p m r", r=PACK),
+                in_=w8_raw[a][:, g, :].bitcast(I32).rearrange("p (m r) -> p m r", r=PACK),
             )
 
         def interleave(dst, src, lo, hi, copy):
@@ -101,67 +114,70 @@ def tile_mix_outl_fm_pl_none_kernel(
             )
 
         def il_x(g, c, lo, hi, copy):
-            interleave(x_bf[(g, c)], x_raw[(g, c)], lo, hi, copy)
+            interleave(x_bf[g][:, tok(c), :], x_raw[(g, c)], lo, hi, copy)
 
-        def deal_w8(g, a):
-            cols = slice(a * 512, (a + 1) * 512)
-            nc.vector.tensor_copy(
-                out=w8[g][:, cols].bitcast(I32).rearrange("p (r m) -> p m r", r=PACK),
-                in_=w8_raw[g][:, cols].bitcast(I32).rearrange("p (m r) -> p m r", r=PACK),
-            )
+        def il_y(a, c, lo, hi, copy):
+            src = y0_f32[c][:] if a == 0 else y1_f32[:, :, tok(c)]
+            interleave(y_bf[a][:, tok(c), :], src, lo, hi, copy)
 
         def quant_x(g, c):
             nc.vector.quantize_mx(
-                out=x_codes[(g, c)][:].bitcast(FP8X4),
-                scales=x_scales[(g, c)][:],
-                in_=x_bf[(g, c)][:].rearrange("p t j -> p (t j)"),
+                out=x_codes[g][:, tok(c)].bitcast(FP8X4),
+                scales=x_scales[g][:, tok(c)],
+                in_=x_bf[g][:, tok(c), :].rearrange("p t j -> p (t j)"),
             )
 
-        def il_y(c, a, lo, hi, copy):
-            interleave(y_bf[(c, a)], y_f32[(c, a)], lo, hi, copy)
-
-        def quant_y(c, a):
+        def quant_y(a, c):
             nc.vector.quantize_mx(
-                out=y_codes[c][:, a, :].bitcast(FP8X4),
+                out=y_codes[a][:, tok(c)].bitcast(FP8X4),
                 scales=y_scales[:, a, tok(c)],
-                in_=y_bf[(c, a)][:].rearrange("p t j -> p (t j)"),
+                in_=y_bf[a][:, tok(c), :].rearrange("p t j -> p (t j)"),
             )
 
-        def matmuls(g, c):
-            for a in range(2):
-                for r in range(PACK):
-                    col = r * 256 + a * P
-                    out = banks[(c, a, r // 2)][:, r % 2, :]
-                    if g >= 2:
-                        for lo in range(0, TC, NB):
-                            nc.tensor.matmul_mx(
-                                out=out[:, lo : lo + NB],
-                                lhsT=w4[g - 2][:, 2 * col : 2 * (col + P)].bitcast(FP4X4),
-                                lhsT_scale=s4[g - 2][:, col : col + P],
-                                rhs=x_codes[(g, c)][:, lo : lo + NB].bitcast(FP8X4),
-                                rhs_scale=x_scales[(g, c)][:, lo : lo + NB],
-                                start=(g == 2 and r % 2 == 0 and lo == 0),
-                                stop=False,
-                            )
-                    else:
-                        nc.tensor.matmul_mx(
-                            out=out,
-                            lhsT=w8[g][:, a * 512 + r * P : a * 512 + (r + 1) * P].bitcast(FP8X4),
-                            lhsT_scale=s8[4 + 4 * g : P, col : col + P],
-                            rhs=x_codes[(g, c)][:].bitcast(FP8X4),
-                            rhs_scale=x_scales[(g, c)][:],
-                            start=False,
-                            stop=(g == 1 and r % 2 == 1),
-                        )
+        def mx(out, g, a, r, lo, hi, start, stop):
+            col = r * 256 + a * P
+            if g >= 2:
+                lhs = w4[g - 2][:, 2 * col : 2 * (col + P)].bitcast(FP4X4)
+                lhs_scale = s4[g - 2][:, col : col + P]
+            else:
+                lhs = w8[(g, a)][:, r * P : (r + 1) * P].bitcast(FP8X4)
+                lhs_scale = s8[4 + 4 * g : P, col : col + P]
+            nc.tensor.matmul_mx(
+                out=out,
+                lhsT=lhs,
+                lhsT_scale=lhs_scale,
+                rhs=x_codes[g][:, lo:hi].bitcast(FP8X4),
+                rhs_scale=x_scales[g][:, lo:hi],
+                start=start,
+                stop=stop,
+            )
 
-        def evac(c, a, h, copy):
-            copy(out=y_f32[(c, a)][:, 2 * h : 2 * h + 2, :], in_=banks[(c, a, h)][:])
+        def matmuls0(g, c):
+            width = NB if g >= 2 else TC
+            for r in range(PACK):
+                for lo in range(0, TC, width):
+                    mx(banks0[(c, r // 2)][:, r % 2, lo : lo + width], g, 0, r, c * TC + lo, c * TC + lo + width,
+                       g == 2 and r % 2 == 0 and lo == 0, g == 1 and r % 2 == 1)
 
-        def store_y(c, a, lo, hi):
-            nc.sync.dma_start(out=y_v[a][:, lo:hi, tok(c)], in_=y_f32[(c, a)][:, lo:hi, :])
+        def matmuls1(passes):
+            for r in range(PACK):
+                for g in passes:
+                    mx(banks1[r][:], g, 1, r, 0, T, g == 2, g == 1)
 
-        def store_codes(c, lo, hi):
-            nc.sync.dma_start(out=codes_v[:, lo:hi, tok(c)], in_=y_codes[c][:, lo:hi, :].bitcast(I32))
+        def evac0(c, h, copy):
+            copy(out=y0_f32[c][:, 2 * h : 2 * h + 2, :], in_=banks0[(c, h)][:])
+
+        def evac1(r, copy):
+            copy(out=y1_f32[:, r, :], in_=banks1[r][:])
+
+        def store_y0(c, lo, hi):
+            nc.sync.dma_start(out=y_v[0][:, lo:hi, tok(c)], in_=y0_f32[c][:, lo:hi, :])
+
+        def store_y1(lo, hi):
+            nc.sync.dma_start(out=y_v[1][:, lo:hi, :], in_=y1_f32[:, lo:hi, :])
+
+        def store_codes(a):
+            nc.sync.dma_start(out=codes_v[a], in_=y_codes[a][:].bitcast(I32))
 
         def store_scales():
             view = y_scales[:].bitcast(I32)
@@ -174,82 +190,81 @@ def tile_mix_outl_fm_pl_none_kernel(
 
         with tc.manual_schedule():
             load_w4(0)
-            load_x(2, 0)
-            il_x(2, 0, 96, 256, s_copy)
+            load_x_full(2)
+            il_x(2, 1, 0, 256, s_copy)
             nc.vector.memset(s4_raw[:].bitcast(I32), 0)
             nc.vector.memset(s8_raw[:].bitcast(I32), 0)
-            deal(w4[0][:], w4_raw[0][:], 2)
-            il_x(2, 0, 0, 96, v_copy)
+            deal_w4(0)
+            il_x(2, 0, 0, 256, v_copy)
             load_s4(nc.sync)
-            load_x(2, 1)
-            load_x(3, 0)
             load_w4(1)
+            load_x_full(3)
             load_s8(nc.sync)
-            load_x(0, 0)
-            load_x(1, 0)
+            load_x_full(0)
             load_w8(0)
+            load_x_half(0)
+            load_x_half(1)
             load_w8(1)
-            load_x(3, 1)
-            load_x(0, 1)
-            load_x(1, 1)
-            il_x(2, 1, 0, 256, s_copy)
             il_x(3, 0, 0, 256, s_copy)
-            il_x(0, 0, 0, 256, s_copy)
-            il_x(1, 0, 0, 256, s_copy)
             il_x(3, 1, 128, 256, s_copy)
-            deal1(s4[0][:], s4_raw[:, 0, :])
+            il_x(0, 1, 64, 256, s_copy)
+            il_x(1, 0, 160, 256, s_copy)
+            il_x(1, 1, 160, 256, s_copy)
+            deal_scales(s4[0][:], s4_raw[:, 0, :])
             quant_x(2, 0)
-            deal1(s4[1][:], s4_raw[:, 1, :])
+            deal_scales(s4[1][:], s4_raw[:, 1, :])
             quant_x(2, 1)
-            deal(w4[1][:], w4_raw[1][:], 2)
+            deal_w4(1)
+            il_x(3, 1, 0, 128, v_copy)
+            deal_scales(s8[:], s8_raw[:])
             quant_x(3, 0)
-            deal1(s8[:], s8_raw[:])
+            quant_x(3, 1)
+            il_x(0, 0, 0, 256, v_copy)
+            il_x(0, 1, 0, 64, v_copy)
             quant_x(0, 0)
             deal_w8(0, 0)
-            deal_w8(0, 1)
-            quant_x(1, 0)
-            deal_w8(1, 0)
-            deal_w8(1, 1)
-            il_x(3, 1, 0, 128, v_copy)
-            matmuls(2, 0)
-            matmuls(2, 1)
-            matmuls(3, 0)
-            matmuls(0, 0)
-            matmuls(1, 0)
-            evac(0, 0, 0, s_copy)
-            evac(0, 1, 1, s_copy)
-            evac(0, 1, 0, s_copy)
-            evac(0, 0, 1, v_copy)
-            quant_x(3, 1)
-            il_x(0, 1, 0, 256, v_copy)
-            il_y(0, 0, 0, 160, v_copy)
             quant_x(0, 1)
-            il_x(1, 1, 0, 256, v_copy)
+            il_x(1, 0, 0, 160, v_copy)
+            deal_w8(1, 0)
+            quant_x(1, 0)
+            il_x(1, 1, 0, 160, v_copy)
             quant_x(1, 1)
-            store_y(0, 0, 0, 4)
-            store_y(0, 1, 0, 4)
-            matmuls(3, 1)
-            matmuls(0, 1)
-            matmuls(1, 1)
-            il_y(0, 0, 160, 256, s_copy)
-            il_y(0, 1, 0, 256, s_copy)
-            evac(1, 0, 0, s_copy)
-            evac(1, 1, 0, s_copy)
+            deal_w8(0, 1)
+            deal_w8(1, 1)
+            matmuls0(2, 0)
+            matmuls0(2, 1)
+            matmuls1([2])
+            matmuls0(3, 0)
+            matmuls0(3, 1)
+            matmuls1([3])
+            matmuls0(0, 0)
+            matmuls0(0, 1)
+            matmuls0(1, 0)
+            matmuls0(1, 1)
+            matmuls1([0, 1])
+            evac0(0, 0, s_copy)
+            evac0(0, 1, s_copy)
+            evac0(1, 1, s_copy)
+            evac1(0, s_copy)
+            evac1(1, s_copy)
+            evac1(2, s_copy)
+            evac0(1, 0, v_copy)
+            il_y(0, 0, 0, 256, v_copy)
+            il_y(0, 1, 0, 256, v_copy)
             quant_y(0, 0)
+            evac1(3, v_copy)
             quant_y(0, 1)
-            evac(1, 0, 1, v_copy)
-            evac(1, 1, 1, v_copy)
-            il_y(1, 0, 0, 160, v_copy)
-            il_y(1, 1, 0, 128, v_copy)
-            store_codes(0, 0, 2)
-            store_y(1, 0, 0, 2)
-            store_y(1, 0, 2, 4)
-            store_y(1, 1, 2, 4)
-            store_y(1, 1, 0, 2)
-            il_y(1, 0, 160, 256, s_copy)
-            il_y(1, 1, 128, 256, s_copy)
+            il_y(1, 0, 0, 256, v_copy)
+            il_y(1, 1, 0, 64, v_copy)
             quant_y(1, 0)
+            store_y0(0, 0, 2)
+            store_y0(0, 2, 4)
+            store_y0(1, 0, 2)
+            store_y0(1, 2, 4)
+            store_y1(0, 2)
+            store_y1(2, 4)
+            store_codes(0)
+            il_y(1, 1, 64, 256, s_copy)
             quant_y(1, 1)
-            store_codes(1, 0, 1)
-            store_codes(1, 1, 2)
+            store_codes(1)
             store_scales()

@@ -189,17 +189,17 @@ def tile_mix_outl_fm_pl_none_kernel(
         v_copy = nc.vector.tensor_copy
 
         with tc.manual_schedule():
+            nc.gpsimd.memset(s8_raw[:].bitcast(I32), 0)
+            load_s8(nc.gpsimd)
             load_w4(0)
             load_x_full(2)
             il_x(2, 1, 0, 256, s_copy)
             nc.vector.memset(s4_raw[:].bitcast(I32), 0)
-            nc.vector.memset(s8_raw[:].bitcast(I32), 0)
             deal_w4(0)
             il_x(2, 0, 0, 256, v_copy)
             load_s4(nc.sync)
             load_w4(1)
             load_x_full(3)
-            load_s8(nc.sync)
             load_x_full(0)
             load_w8(0)
             load_x_half(0)

from contextlib import ExitStack

import concourse.mybir as mybir

K, M, T = 2048, 1024, 512
FLOPS = 2 * K * M * T

F32 = mybir.dt.float32
BF16 = mybir.dt.bfloat16
I32 = mybir.dt.int32
U32 = mybir.dt.uint32
U8 = mybir.dt.uint8
FP8X4 = mybir.dt.float8_e4m3fn_x4
FP4X4 = mybir.dt.float4_e2m1fn_x4

P = 128
PACK = 4
TC = 256
NB = 128
NA = 512


def tile_mix_outl_fm_pl_none_kernel(
    tc, x, w8_words, w8_scales, w4_words, w4_scales, out_0, out_1, out_2
):
    nc = tc.nc
    x_v = x.rearrange("(g p j) t -> g p j t", p=P, j=PACK)
    y_v = out_0.rearrange("(a p r) t -> a p r t", p=P, r=PACK)
    w8_v = w8_words.rearrange("g p n i -> p g (n i)").bitcast(I32)
    w4_v = w4_words.bitcast(I32)
    s8_v = w8_scales.bitcast(I32)
    s4_v = w4_scales.bitcast(I32).rearrange("g (q r) n -> r q g n", r=4)
    codes_v = out_1.rearrange("a p t i -> a p (t i)").bitcast(I32)
    scales_v = out_2.bitcast(I32).rearrange("a (q r) t -> r q a t", r=4)

    with ExitStack() as ctx:
        sb = ctx.enter_context(tc.tile_pool(name="sb", bufs=1))
        ps = ctx.enter_context(tc.psum_pool(name="ps", bufs=1))

        def sbt(shape, dtype, name):
            return sb.tile(shape, dtype, name=name, align_bytes=64)

        def tok(c):
            return slice(c * TC, (c + 1) * TC)

        pairs = [(i, j) for i in range(2) for j in range(2)]
        w4_raw = [sbt([P, 2 * M], U8, "w4_raw%d" % g) for g in range(2)]
        w4 = [sbt([P, 2 * M], U8, "w4_%d" % g) for g in range(2)]
        w8_raw = [sbt([P, 2, NA], U32, "w8_raw%d" % a) for a in range(2)]
        w8 = {k: sbt([P, NA], U32, "w8_%d%d" % k) for k in pairs}
        s4_raw = sbt([P, 2, M], U8, "s4_raw")
        s4 = [sbt([P, M], U8, "s4_%d" % g) for g in range(2)]
        s8_raw = sbt([P, M], U8, "s8_raw")
        s8 = sbt([P, M], U8, "s8")
        x_full = {g: sbt([P, PACK, T], F32, "x_full%d" % g) for g in (0, 2, 3)}
        x_half = [sbt([P, PACK, TC], F32, "x_half%d" % c) for c in range(2)]
        x_raw = {(g, c): x_full[g][:, :, tok(c)] for g in x_full for c in range(2)}
        x_raw = dict(list(x_raw.items()) + [((1, c), x_half[c][:]) for c in range(2)])
        x_bf = [sbt([P, T, PACK], BF16, "x_bf%d" % g) for g in range(4)]
        x_codes = [sbt([P, T], U32, "x_codes%d" % g) for g in range(4)]
        x_scales = [sbt([P, T], U8, "x_scales%d" % g) for g in range(4)]
        y0_f32 = [sbt([P, PACK, TC], F32, "y0_f32%d" % c) for c in range(2)]
        y1_f32 = sbt([P, PACK, T], F32, "y1_f32")
        y_bf = [sbt([P, T, PACK], BF16, "y_bf%d" % a) for a in range(2)]
        y_codes = [sbt([P, T], U32, "y_codes%d" % a) for a in range(2)]
        y_scales = sbt([P, 2, T], U8, "y_scales")
        banks0 = {k: ps.tile([P, 2, TC], F32, name="bank0_%d%d" % k) for k in pairs}
        banks1 = [ps.tile([P, T], F32, name="bank1_%d" % r) for r in range(PACK)]

        def load_x_full(g):
            nc.sync.dma_start(out=x_full[g][:], in_=x_v[g])

        def load_x_half(c):
            nc.sync.dma_start(out=x_half[c][:], in_=x_v[1][:, :, tok(c)])

        def load_w4(g):
            nc.sync.dma_start(out=w4_raw[g][:].bitcast(I32), in_=w4_v[g])

        def load_w8(a):
            nc.sync.dma_start(out=w8_raw[a][:].bitcast(I32), in_=w8_v[:, :, a * NA : (a + 1) * NA])

        def load_s4(eng):
            view = s4_raw[:].bitcast(I32)
            for r in range(4):
                eng.dma_start(out=view[r:P:32], in_=s4_v[r])

        def load_s8(eng):
            view = s8_raw[:].bitcast(I32)
            for q in range(4):
                eng.dma_start(out=view[32 * q + 4 : 32 * q + 12, :], in_=s8_v[:, 4 * q : 4 * q + 4, :])

        def deal_w4(g):
            nc.vector.tensor_copy(
                out=w4[g][:].rearrange("p (r m b) -> p r m b", r=PACK, b=2),
                in_=w4_raw[g][:].rearrange("p (m r b) -> p r m b", r=PACK, b=2),
            )

        def deal_scales(dst, src):
            nc.vector.tensor_copy(
                out=dst.rearrange("p (r m) -> p r m", r=PACK),
                in_=src.rearrange("p (m r) -> p r m", r=PACK),
            )

        def deal_w8(g, a):
            nc.vector.tensor_copy(
                out=w8[(g, a)][:].bitcast(I32).rearrange("p (r m) -> p m r", r=PACK),
                in_=w8_raw[a][:, g, :].bitcast(I32).rearrange("p (m r) -> p m r", r=PACK),
            )

        def interleave(dst, src, lo, hi, copy):
            copy(
                out=dst[:, lo:hi, :].rearrange("p (c i) j -> p c j i", i=2),
                in_=src[:, :, lo:hi].rearrange("p j (c i) -> p c j i", i=2),
            )

        def il_x(g, c, lo, hi, copy):
            interleave(x_bf[g][:, tok(c), :], x_raw[(g, c)], lo, hi, copy)

        def il_y(a, c, lo, hi, copy):
            src = y0_f32[c][:] if a == 0 else y1_f32[:, :, tok(c)]
            interleave(y_bf[a][:, tok(c), :], src, lo, hi, copy)

        def quant_x(g, c):
            nc.vector.quantize_mx(
                out=x_codes[g][:, tok(c)].bitcast(FP8X4),
                scales=x_scales[g][:, tok(c)],
                in_=x_bf[g][:, tok(c), :].rearrange("p t j -> p (t j)"),
            )

        def quant_y(a, c):
            nc.vector.quantize_mx(
                out=y_codes[a][:, tok(c)].bitcast(FP8X4),
                scales=y_scales[:, a, tok(c)],
                in_=y_bf[a][:, tok(c), :].rearrange("p t j -> p (t j)"),
            )

        def mx(out, g, a, r, lo, hi, start, stop):
            col = r * 256 + a * P
            if g >= 2:
                lhs = w4[g - 2][:, 2 * col : 2 * (col + P)].bitcast(FP4X4)
                lhs_scale = s4[g - 2][:, col : col + P]
            else:
                lhs = w8[(g, a)][:, r * P : (r + 1) * P].bitcast(FP8X4)
                lhs_scale = s8[4 + 4 * g : P, col : col + P]
            nc.tensor.matmul_mx(
                out=out,
                lhsT=lhs,
                lhsT_scale=lhs_scale,
                rhs=x_codes[g][:, lo:hi].bitcast(FP8X4),
                rhs_scale=x_scales[g][:, lo:hi],
                start=start,
                stop=stop,
            )

        def matmuls0(g, c):
            width = NB if g >= 2 else TC
            for r in range(PACK):
                for lo in range(0, TC, width):
                    mx(banks0[(c, r // 2)][:, r % 2, lo : lo + width], g, 0, r, c * TC + lo, c * TC + lo + width,
                       g == 2 and r % 2 == 0 and lo == 0, g == 1 and r % 2 == 1)

        def matmuls1(passes):
            for r in range(PACK):
                for g in passes:
                    mx(banks1[r][:], g, 1, r, 0, T, g == 2, g == 1)

        def evac0(c, h, copy):
            copy(out=y0_f32[c][:, 2 * h : 2 * h + 2, :], in_=banks0[(c, h)][:])

        def evac1(r, copy):
            copy(out=y1_f32[:, r, :], in_=banks1[r][:])

        def store_y0(c, lo, hi):
            nc.sync.dma_start(out=y_v[0][:, lo:hi, tok(c)], in_=y0_f32[c][:, lo:hi, :])

        def store_y1(lo, hi):
            nc.sync.dma_start(out=y_v[1][:, lo:hi, :], in_=y1_f32[:, lo:hi, :])

        def store_codes(a):
            nc.sync.dma_start(out=codes_v[a], in_=y_codes[a][:].bitcast(I32))

        def store_scales():
            view = y_scales[:].bitcast(I32)
            for r in range(4):
                eng = nc.scalar if r % 2 == 0 else nc.sync
                eng.dma_start(out=scales_v[r], in_=view[r:P:32])

        s_copy = nc.scalar.copy
        v_copy = nc.vector.tensor_copy

        with tc.manual_schedule():
            nc.gpsimd.memset(s8_raw[:].bitcast(I32), 0)
            load_s8(nc.gpsimd)
            load_w4(0)
            load_x_full(2)
            il_x(2, 1, 0, 256, s_copy)
            nc.vector.memset(s4_raw[:].bitcast(I32), 0)
            deal_w4(0)
            il_x(2, 0, 0, 256, v_copy)
            load_s4(nc.sync)
            load_w4(1)
            load_x_full(3)
            load_x_full(0)
            load_w8(0)
            load_x_half(0)
            load_x_half(1)
            load_w8(1)
            il_x(3, 0, 0, 256, s_copy)
            il_x(3, 1, 128, 256, s_copy)
            il_x(0, 1, 64, 256, s_copy)
            il_x(1, 0, 160, 256, s_copy)
            il_x(1, 1, 160, 256, s_copy)
            deal_scales(s4[0][:], s4_raw[:, 0, :])
            quant_x(2, 0)
            deal_scales(s4[1][:], s4_raw[:, 1, :])
            quant_x(2, 1)
            deal_w4(1)
            il_x(3, 1, 0, 128, v_copy)
            deal_scales(s8[:], s8_raw[:])
            quant_x(3, 0)
            quant_x(3, 1)
            il_x(0, 0, 0, 256, v_copy)
            il_x(0, 1, 0, 64, v_copy)
            quant_x(0, 0)
            deal_w8(0, 0)
            quant_x(0, 1)
            il_x(1, 0, 0, 160, v_copy)
            deal_w8(1, 0)
            quant_x(1, 0)
            il_x(1, 1, 0, 160, v_copy)
            quant_x(1, 1)
            deal_w8(0, 1)
            deal_w8(1, 1)
            matmuls0(2, 0)
            matmuls0(2, 1)
            matmuls1([2])
            matmuls0(3, 0)
            matmuls0(3, 1)
            matmuls1([3])
            matmuls0(0, 0)
            matmuls0(0, 1)
            matmuls0(1, 0)
            matmuls0(1, 1)
            matmuls1([0, 1])
            evac0(0, 0, s_copy)
            evac0(0, 1, s_copy)
            evac0(1, 1, s_copy)
            evac1(0, s_copy)
            evac1(1, s_copy)
            evac1(2, s_copy)
            evac0(1, 0, v_copy)
            il_y(0, 0, 0, 256, v_copy)
            il_y(0, 1, 0, 256, v_copy)
            quant_y(0, 0)
            evac1(3, v_copy)
            quant_y(0, 1)
            il_y(1, 0, 0, 256, v_copy)
            il_y(1, 1, 0, 64, v_copy)
            quant_y(1, 0)
            store_y0(0, 0, 2)
            store_y0(0, 2, 4)
            store_y0(1, 0, 2)
            store_y0(1, 2, 4)
            store_y1(0, 2)
            store_y1(2, 4)
            store_codes(0)
            il_y(1, 1, 64, 256, s_copy)
            quant_y(1, 1)
            store_codes(1)
            store_scales()
